import numpy as np
import ml_dtypes


def mxq(x, axis, fmt="e4m3"):
    dtype, down = {"e4m3": (ml_dtypes.float8_e4m3fn, 7), "e5m2": (ml_dtypes.float8_e5m2, 14)}[fmt]
    v = np.moveaxis(np.asarray(x, np.float32).astype(ml_dtypes.bfloat16).astype(np.float64), axis, -1)
    blocks = v.reshape(v.shape[:-1] + (-1, 32))
    amax = np.abs(blocks).max(-1, keepdims=True)
    byte = np.maximum(np.where(amax > 0, np.frexp(amax)[1] - 1 + 127, 0) - down, 1)
    scale = np.exp2(byte - 127.0)
    codes = (blocks / scale).astype(np.float32).astype(dtype).astype(np.float64)
    return np.moveaxis((codes * scale).reshape(v.shape), -1, axis)


WIDE = False


def mx_kscale(k):
    if not WIDE:
        return np.ones(k)
    levels = np.array([10, -10, 5, -5, 0])
    if k % 512:
        return np.exp2(np.random.permutation(np.resize(levels, k // 32))).repeat(32)
    a = np.empty((k // 512, 16))
    for p in range(k // 512):
        a[p, :8] = np.random.permutation(np.resize(levels, 8))
        for g in range(8):
            far = levels[np.abs(levels - a[p, g]) >= 10]
            a[p, g + 8] = far[np.random.randint(len(far))]
    return np.exp2(a.ravel()).repeat(32)


BF16 = ml_dtypes.bfloat16


def bf(x):
    return np.asarray(x, np.float32).astype(BF16)


def f64(x):
    return np.asarray(x).astype(np.float64)


E2M1 = np.array([0.0, 0.5, 1.0, 1.5, 2.0, 3.0, 4.0, 6.0, -0.0, -0.5, -1.0, -1.5, -2.0, -3.0, -4.0, -6.0])


def pack_weight(w, fmt):
    k, n = w.shape
    w = f64(bf(w)).reshape(k // 32, 32, n)
    amax = np.abs(w).max(1)
    if fmt == "e4m3":
        byte = np.frexp(amax)[1] - 1 + 127 - 7
    else:
        mant, ex = np.frexp(amax / 6.0)
        byte = np.where(mant > 0.5, ex, ex - 1) + 127
    byte = np.clip(np.where(amax > 0, byte, 1), 1, 254)
    scaled = (w * np.exp2(127.0 - byte)[:, None, :]).reshape(k, n).astype(np.float32)
    by_word = np.ascontiguousarray(scaled.reshape(k // 512, 128, 4, n).transpose(0, 1, 3, 2))
    if fmt == "e4m3":
        words = by_word.astype(ml_dtypes.float8_e4m3fn).view(np.uint8)
    else:
        c = by_word.astype(ml_dtypes.float4_e2m1fn).view(np.uint8) & 0xF
        words = c[..., 0::2] | (c[..., 1::2] << 4)
    return np.ascontiguousarray(words), np.ascontiguousarray(byte.astype(np.uint8).reshape(k // 512, 16, n))


def unpack_weight(words, scales, fmt):
    g, p, n, _ = words.shape
    if fmt == "e4m3":
        vals = np.ascontiguousarray(words).view(ml_dtypes.float8_e4m3fn).astype(np.float64)
    else:
        nib = np.empty((g, p, n, 4), np.uint8)
        nib[..., 0::2] = words & 0xF
        nib[..., 1::2] = words >> 4
        vals = E2M1[nib]
    vals = vals * np.repeat(np.exp2(scales.astype(np.float64) - 127.0), 8, axis=1)[..., None]
    return vals.transpose(0, 1, 3, 2).reshape(g * 512, n)
def pack4(w):
    words, scales = pack_weight(w, "e2m1")
    return words.reshape(words.shape[0], 128, -1), scales


def unpack4(words, scales):
    return unpack_weight(words.reshape(words.shape[0], 128, -1, 2), scales, "e2m1")


def planes(Y):
    n, m = Y.shape
    b = f64(bf(Y)).reshape(n // 32, 32, m)
    amax = np.abs(b).max(1)
    byte = np.clip(np.where(amax > 0, np.frexp(amax)[1] - 1 + 127 - 7, 1), 1, 254)
    codes = (b * np.exp2(127.0 - byte)[:, None, :]).reshape(n, m).astype(np.float32).astype(ml_dtypes.float8_e4m3fn).view(np.uint8)
    words = codes.reshape(n // 512, 128, 4, m).transpose(0, 1, 3, 2)
    return np.ascontiguousarray(words), np.ascontiguousarray(byte.astype(np.uint8).reshape(n // 512, 16, m))


U, I, R = 1024, 3072, 512

def setup_inputs():
    noise = np.random.randn
    s = mx_kscale(I)
    t = mx_kscale(R)
    h = noise(U, I)
    enc = noise(I, R) / np.sqrt(I)
    hist_words, hist_scales = pack4(h.T * s[:, None])
    enc_words, enc_scales = pack4(enc / s[:, None] * t[None, :])
    return {
        "hist_words": hist_words,
        "hist_scales": hist_scales,
        "enc_words": enc_words,
        "enc_scales": enc_scales,
        "dec": bf(noise(R, I) / np.sqrt(R) / t[:, None]),
        "user_scale": bf(np.exp(0.3 * noise(U))),
        "code_bias": bf(0.3 * noise(R) * t),
        "history": bf(h),
        "self_weight": bf(0.6 + 0.1 * noise(I)),
        "item_gain": bf(np.exp(0.8 * noise(I))),
        "item_bias": bf(0.3 * noise(I)),
    }

def reference(hist_words, hist_scales, enc_words, enc_scales, dec, user_scale, code_bias, history, self_weight, item_gain, item_bias):
    A = unpack4(hist_words, hist_scales)
    E = unpack4(enc_words, enc_scales)
    H = (A.T @ E) * f64(user_scale)[:, None] + f64(code_bias)[None, :]
    Z = mxq(H, 1, "e4m3") @ mxq(f64(dec), 0, "e4m3")
    y = (Z - f64(history) * f64(self_weight)[None, :]) * f64(item_gain)[None, :] + f64(item_bias)[None, :]
    Y = y.T
    words, scales = planes(Y)
    return y, words, scales

@@ -1,0 +1,397 @@
+from contextlib import ExitStack
+
+import concourse.mybir as mybir
+from concourse.masks import make_identity
+
+U, I, R = 1024, 3072, 512
+FLOPS = 2 * U * I * R * 2
+
+F32 = mybir.dt.float32
+BF16 = mybir.dt.bfloat16
+I32 = mybir.dt.int32
+U32 = mybir.dt.uint32
+U8 = mybir.dt.uint8
+FP8X4 = mybir.dt.float8_e4m3fn_x4
+FP4X4 = mybir.dt.float4_e2m1fn_x4
+MULT = mybir.AluOpType.mult
+ADD = mybir.AluOpType.add
+IDENT = mybir.ActivationFunctionType.Identity
+
+P = 128
+G = 6
+HALF = 512
+UNITS = 12
+N_AY = 3
+N_Y = 5
+N_WORDS = 4
+ROW_GAIN, ROW_SW, ROW_BIAS, ROW_CB, ROW_US = 0, 6, 12, 18, 24
+N_COLS = 19
+
+
+def tile_lowrank_diagonal_item_scores_k5_kernel(
+    tc, hist_words, hist_scales, enc_words, enc_scales, dec, user_scale, code_bias, history,
+    self_weight, item_gain, item_bias, out_0, out_1, out_2,
+):
+    nc = tc.nc
+    with ExitStack() as ctx:
+        sb = ctx.enter_context(tc.tile_pool(name="sb", bufs=1))
+        ps = ctx.enter_context(tc.psum_pool(name="ps", bufs=1))
+
+        def sbuf(name, shape, dtype):
+            return sb.tile(shape, dtype, name=name, align_bytes=64)
+
+        a_words = sbuf("a_words", [P, G, 2 * U], U8)
+        e_words = sbuf("e_words", [P, G, 2 * R], U8)
+        a_scales = sbuf("a_scales", [P, G, U], U8)
+        e_scales = sbuf("e_scales", [P, G, R], U8)
+        dec_raw = sbuf("dec_raw", [P, 4, I], BF16)
+        dec_stage = [sbuf("dec_stage%d" % n, [P, 4 * HALF], BF16) for n in range(2)]
+        dec_codes = sbuf("dec_codes", [P, G, HALF], U32)
+        dec_scales = sbuf("dec_scales", [P, G, HALF], U8)
+        hist = sbuf("hist", [P, 8, I], BF16)
+        h_rows = [sbuf("h_rows%d" % n, [P, R], BF16) for n in range(4)]
+        h_stage = sbuf("h_stage", [P, 4 * HALF], BF16)
+        h_codes = sbuf("h_codes", [P, U], U32)
+        h_scales = sbuf("h_scales", [P, U], U8)
+        yt = [sbuf("yt%d" % n, [P, 4, HALF], F32) for n in range(N_AY)]
+        y_stage = [sbuf("y_stage%d" % n, [P, 4 * HALF], BF16) for n in range(3)]
+        y_words = [sbuf("y_words%d" % n, [P, HALF], U32) for n in range(N_WORDS)]
+        y_scales = [sbuf("y_scales%d" % n, [P, HALF], U8) for n in range(4)]
+        y_rows = [sbuf("y_rows%d" % n, [P, 4, HALF], F32) for n in range(N_Y)]
+        ident = sbuf("ident", [P, P], F32)
+        vec = sbuf("vec", [P, HALF], BF16)
+        vec32 = sbuf("vec32", [P, 5 * P], F32)
+        cols = sbuf("cols", [P, 4, N_COLS], F32)
+        neg_c = sbuf("neg_c", [P, 4, G], F32)
+        us_col = sbuf("us_col", [P, 8], F32)
+        cb_rows = sbuf("cb_rows", [P, R], F32)
+        banks = [ps.tile([P, HALF], F32, name="bank%d" % n) for n in range(8)]
+        bank_of = {}
+
+        def take(key):
+            bank_of[key] = banks.pop(0)
+            return bank_of[key]
+
+        def give(key):
+            banks.append(bank_of[key])
+
+        ctx.enter_context(tc.manual_schedule())
+
+        def load_words(tile, src, gs, c0, c1):
+            nc.sync.dma_start(out=tile[:, gs, c0:c1].bitcast(I32),
+                              in_=src[gs, :, c0:c1].rearrange("g p n -> p g n").bitcast(I32))
+
+        def load_scales(eng, tile, src, r, c0, c1):
+            eng.dma_start(out=tile[r:P:32, :, c0:c1].bitcast(I32),
+                          in_=src.rearrange("g (q r) n -> r q g n", r=4)[r][:, :, c0:c1].bitcast(I32))
+
+        def load_dec(g0, g1):
+            c = slice(g0 * HALF, g1 * HALF)
+            nc.sync.dma_start(out=dec_raw[:, :, c], in_=dec[:, c].rearrange("(p j) c -> p j c", j=4))
+
+        def load_hist(j0, j1, c0, c1):
+            nc.sync.dma_start(out=hist[:, j0:j1, c0:c1],
+                              in_=history[j0 * P:j1 * P, c0:c1].rearrange("(j q) c -> q j c", q=P))
+
+        nc.vector.memset(vec[:].bitcast(I32), 0)
+        nc.vector.memset(e_scales[:].rearrange("p g n -> p (g n)").bitcast(I32), 0)
+        nc.vector.memset(a_scales[:, :, 0:HALF].bitcast(I32), 0)
+        nc.vector.memset(a_scales[:, :, HALF:U].bitcast(I32), 0)
+        load_words(e_words, enc_words, slice(0, 1), 0, 2 * R)
+        load_words(a_words, hist_words, slice(0, 1), 0, U)
+        nc.gpsimd.dma_start(out=vec[ROW_CB:ROW_CB + 1, :], in_=code_bias.rearrange("(o n) -> o n", o=1))
+        nc.gpsimd.dma_start(out=vec[ROW_US:ROW_US + 8, 0:P], in_=user_scale.rearrange("(j q) -> j q", q=P))
+        for row, src in ((ROW_GAIN, item_gain), (ROW_SW, self_weight), (ROW_BIAS, item_bias)):
+            nc.gpsimd.dma_start(out=vec[row:row + G, :], in_=src.rearrange("(g n) -> g n", n=HALF))
+        make_identity(nc, ident[:])
+        for r in range(4):
+            load_scales(nc.sync, e_scales, enc_scales, r, 0, R)
+        for r in range(4):
+            load_scales(nc.sync, a_scales, hist_scales, r, 0, HALF)
+        for gs in (slice(1, 3), slice(3, 6)):
+            load_words(e_words, enc_words, gs, 0, 2 * R)
+            load_words(a_words, hist_words, gs, 0, U)
+        for r in range(4):
+            load_scales(nc.gpsimd, a_scales, hist_scales, r, HALF, U)
+        load_dec(0, 2)
+        load_hist(0, 4, 0, 1024)
+        load_hist(0, 4, 1024, 2048)
+        load_words(a_words, hist_words, slice(0, 6), U, 2 * U)
+        load_dec(2, 4)
+        load_hist(0, 4, 2048, I)
+        load_dec(4, 6)
+        for j in range(4, 8):
+            load_hist(j, j + 1, 0, I)
+
+        def encode(j, gs):
+            if gs[0] == 0:
+                take(("enc", j))
+            for g in gs:
+                nc.tensor.matmul_mx(
+                    out=bank_of["enc", j][:], lhsT=a_words[:, g, 2 * P * j:2 * P * (j + 1)].bitcast(FP4X4),
+                    lhsT_scale=a_scales[:, g, P * j:P * (j + 1)], rhs=e_words[:, g, :].bitcast(FP4X4),
+                    rhs_scale=e_scales[:, g, :], start=(g == 0), stop=(g == G - 1))
+
+        def h_finish(j):
+            src = bank_of["enc", j][:].rearrange("q (p u e) -> q u p e", u=2, e=2)
+            for u in range(2):
+                c = slice(256 * u, 256 * (u + 1))
+                nc.vector.scalar_tensor_tensor(
+                    out=h_rows[j % 4][:, c].rearrange("q (p e) -> q p e", e=2), in0=src[:, u],
+                    scalar=us_col[:, j:j + 1], in1=cb_rows[:, c].rearrange("q (p e) -> q p e", e=2),
+                    op0=MULT, op1=ADD)
+            give(("enc", j))
+
+        def h_turn(j):
+            bank = take(("ht", j))
+            for u in range(2):
+                nc.tensor.transpose(bank[:, P * u:P * (u + 1)], h_rows[j % 4][:].bitcast(F32)[:, P * u:P * (u + 1)], ident[:])
+
+        def h_copy(j, copy=nc.scalar.copy):
+            c = slice(HALF * (j % 4), HALF * (j % 4 + 1))
+            copy(out=h_stage[:, c].bitcast(F32).rearrange("p (r u) -> p r u", u=2),
+                           in_=bank_of["ht", j][:, 0:2 * P].rearrange("p (u r) -> p r u", u=2))
+            give(("ht", j))
+
+        def h_quant(j):
+            c = slice(HALF * (j % 4), HALF * (j % 4 + 1))
+            nc.vector.quantize_mx(out=h_codes[:, P * j:P * (j + 1)].bitcast(FP8X4),
+                                  scales=h_scales[:, P * j:P * (j + 1)], in_=h_stage[:, c])
+
+        def dec_lay(g, eng, t0=0, t1=4):
+            dst = dec_stage[g % 2][:].rearrange("p (t m j) -> p t m j", t=4, j=4)[:, t0:t1]
+            src = dec_raw[:, :, g * HALF:(g + 1) * HALF].rearrange("p j (m t) -> p t m j", t=4)[:, t0:t1]
+            if eng == "pool":
+                nc.gpsimd.tensor_scalar(out=dst, in0=src, scalar1=1.0, scalar2=0.0, op0=MULT, op1=ADD)
+            elif eng == "act":
+                nc.scalar.copy(out=dst, in_=src)
+            else:
+                nc.vector.tensor_copy(out=dst, in_=src)
+
+        def dec_quant(g):
+            nc.vector.quantize_mx(out=dec_codes[:, g, :].bitcast(FP8X4), scales=dec_scales[:, g, :], in_=dec_stage[g % 2][:])
+
+        def hist_turn(i, u):
+            h, g = divmod(i, G)
+            bank = take(("hist", i, u))
+            words = hist[:].bitcast(F32)
+            for j in range(4):
+                nc.tensor.transpose(bank[:, P * j:P * (j + 1)], words[:, 4 * h + j, 256 * g + u:256 * (g + 1):2], ident[:])
+
+        def self_term(i, t, eng="act"):
+            g = i % G
+            src = bank_of["hist", i, t // 2][:].bitcast(BF16)[:, t % 2:2 * HALF:2]
+            dst = yt[i % N_AY][:, t, :]
+            if eng == "act":
+                nc.scalar.activation(out=dst, in_=src, func=IDENT, bias=cols[:, t, ROW_BIAS + g:ROW_BIAS + g + 1],
+                                     scale=neg_c[:, t, g:g + 1])
+            else:
+                nc.vector.tensor_scalar(out=dst, in0=src, scalar1=neg_c[:, t, g:g + 1],
+                                        scalar2=cols[:, t, ROW_BIAS + g:ROW_BIAS + g + 1], op0=MULT, op1=ADD)
+            if t % 2 == 1:
+                give(("hist", i, t // 2))
+
+        def decode(i, t):
+            h, g = divmod(i, G)
+            nc.tensor.matmul_mx(
+                out=take(("z", i, t))[:], lhsT=dec_codes[:, g, P * t:P * (t + 1)].bitcast(FP8X4),
+                lhsT_scale=dec_scales[:, g, P * t:P * (t + 1)], rhs=h_codes[:, HALF * h:HALF * (h + 1)].bitcast(FP8X4),
+                rhs_scale=h_scales[:, HALF * h:HALF * (h + 1)], start=True, stop=True)
+
+        def finish(i, t):
+            g = i % G
+            dst = yt[i % N_AY][:, t, :]
+            nc.vector.scalar_tensor_tensor(out=dst, in0=bank_of["z", i, t][:], scalar=cols[:, t, ROW_GAIN + g:ROW_GAIN + g + 1],
+                                           in1=dst, op0=MULT, op1=ADD)
+            give(("z", i, t))
+
+        def y_turn(i, j):
+            bank = take(("y", i, j))
+            for t in range(4):
+                nc.tensor.transpose(bank[:, P * t:P * (t + 1)], yt[i % N_AY][:, t, P * j:P * (j + 1)], ident[:])
+
+        def y_copy(i, j, eng):
+            dst = y_rows[i % N_Y][:, j, :].rearrange("q (p t) -> q p t", t=4)
+            src = bank_of["y", i, j][:].rearrange("q (t p) -> q p t", t=4)
+            if eng == "act":
+                nc.scalar.copy(out=dst, in_=src)
+            else:
+                nc.vector.tensor_copy(out=dst, in_=src)
+            give(("y", i, j))
+
+        def y_round(i, m0=0, m1=HALF, eng="pool"):
+            dst = y_stage[i % 3][:, 4 * m0:4 * m1].rearrange("p (m t) -> p m t", t=4)
+            src = yt[i % N_AY][:, :, m0:m1].rearrange("p t m -> p m t")
+            if eng == "pool":
+                nc.gpsimd.tensor_scalar(out=dst, in0=src, scalar1=1.0, scalar2=0.0, op0=MULT, op1=ADD)
+            elif eng == "act":
+                nc.scalar.copy(out=dst, in_=src)
+            else:
+                nc.vector.tensor_copy(out=dst, in_=src)
+
+        def y_quant(i, m0=0, m1=HALF):
+            h, g = divmod(i, G)
+            nc.vector.quantize_mx(out=y_words[i % N_WORDS][:, m0:m1].bitcast(FP8X4),
+                                  scales=y_scales[2 * h + g // 4][4 * (g % 4):P, m0:m1], in_=y_stage[i % 3][:, 4 * m0:4 * m1])
+
+        def store_y(i, j0, j1):
+            h, g = divmod(i, G)
+            nc.sync.dma_start(
+                out=out_0[HALF * h + P * j0:HALF * h + P * j1, HALF * g:HALF * (g + 1)].rearrange("(j q) c -> q j c", q=P),
+                in_=y_rows[i % N_Y][:, j0:j1, :])
+
+        def store_words(i, m0=0, m1=HALF):
+            h, g = divmod(i, G)
+            nc.sync.dma_start(
+                out=out_1[g].rearrange("p m t -> p (m t)")[:, 4 * (HALF * h + m0):4 * (HALF * h + m1)].bitcast(I32),
+                in_=y_words[i % N_WORDS][:, m0:m1].bitcast(I32))
+
+        def store_scales(h, part):
+            g0, n = (0, 4) if part == 0 else (4, 2)
+            for q in range(4):
+                nc.sync.dma_start(out=out_2[g0:g0 + n, 4 * q:4 * q + 4, HALF * h:HALF * (h + 1)].bitcast(I32),
+                                  in_=y_scales[2 * h + part][32 * q:32 * q + 4 * n, :].bitcast(I32))
+
+        for g in (0, 1):
+            for j in range(4):
+                encode(j, [g])
+        nc.vector.tensor_copy(out=vec32[:, 0:HALF].rearrange("r (t m) -> r t m", t=4), in_=vec[:].rearrange("r (m t) -> r t m", t=4))
+        nc.vector.tensor_copy(out=vec32[:, HALF:], in_=vec[:, 0:P])
+        vb, ub = take("vec"), take("us")
+        for t in range(4):
+            nc.tensor.transpose(vb[:, P * t:P * (t + 1)], vec32[:, P * t:P * (t + 1)], ident[:])
+        nc.tensor.transpose(ub[:, 0:P], vec32[:, HALF:], ident[:])
+        nc.vector.tensor_copy(out=cols[:], in_=vb[:].rearrange("p (t r) -> p t r", t=4)[:, :, 0:N_COLS])
+        nc.vector.tensor_copy(out=us_col[:], in_=ub[:, ROW_US:ROW_US + 8])
+        give("vec")
+        give("us")
+        nc.vector.scalar_tensor_tensor(out=neg_c[:], in0=cols[:, :, ROW_SW:ROW_SW + G], scalar=-1.0,
+                                       in1=cols[:, :, ROW_GAIN:ROW_GAIN + G], op0=MULT, op1=MULT)
+        for j in range(4):
+            encode(j, [2])
+        cbb = take("cb")
+        for t in range(4):
+            nc.tensor.transpose(cbb[:, P * t:P * (t + 1)], cols[:, t, ROW_CB:ROW_CB + 1].to_broadcast([P, P]), ident[:])
+        nc.scalar.activation(out=cb_rows[:].rearrange("q (u p e) -> q u p e", u=2, e=2),
+                             in_=cbb[:].rearrange("q (u e p) -> q u p e", u=2, e=2), func=IDENT)
+        give("cb")
+        encode(0, [3, 4, 5])
+        encode(1, [3, 4, 5])
+        h_finish(0)
+        encode(2, [3, 4, 5])
+        h_finish(1)
+        dec_lay(0, "dve")
+        dec_lay(1, "act", 0, 2)
+        h_turn(0)
+        h_turn(1)
+        h_copy(0)
+        h_copy(1)
+        dec_lay(1, "act", 2, 4)
+        encode(3, [3, 4, 5])
+        h_finish(2)
+        h_quant(0)
+        h_finish(3)
+        h_quant(1)
+        dec_quant(0)
+        h_turn(2)
+        h_copy(2)
+        hist_turn(0, 0)
+        h_turn(3)
+        h_copy(3)
+        hist_turn(0, 1)
+        h_quant(2)
+        h_quant(3)
+        dec_quant(1)
+        for t in range(4):
+            self_term(0, t)
+
+        for i in range(UNITS):
+            nxt = 2 if i == 0 else (i + 1 if 2 <= i < UNITS - 1 else None)
+            mixed = 1 <= i <= 4
+            if mixed:
+                encode(3 + i, list(range(G)))
+            if i == 1 or i >= 3:
+                self_term(2 if i == 1 else i, 2)
+                self_term(2 if i == 1 else i, 3)
+            if mixed:
+                dec_lay(i + 1, "act", 2, 4)
+                h_finish(3 + i)
+            for t in range(4):
+                decode(i, t)
+            if i == 0:
+                for u in range(2):
+                    hist_turn(1, u)
+                for t in range(4):
+                    self_term(1, t)
+            finish(i, 0)
+            finish(i, 1)
+            if mixed:
+                h_turn(3 + i)
+                h_copy(3 + i)
+            if i >= 1:
+                y_turn(i - 1, 0)
+                y_turn(i - 1, 1)
+            finish(i, 2)
+            if i >= 1:
+                y_copy(i - 1, 0, "act")
+            if nxt:
+                hist_turn(nxt, 0)
+            if mixed:
+                dec_lay(i + 1, "dve", 0, 2)
+                h_quant(3 + i)
+                dec_quant(i + 1)
+            if i == 10:
+                y_quant(8)
+                y_quant(9)
+            if not mixed:
+                finish(i, 3)
+            if i >= 1:
+                y_copy(i - 1, 1, "act")
+                y_turn(i - 1, 2)
+                y_turn(i - 1, 3)
+            if mixed:
+                finish(i, 3)
+            if 2 <= i <= 9:
+                y_quant(i - 2)
+            if i < 10:
+                y_round(i)
+            if i == 10:
+                y_round(i, 0, 256)
+                y_round(i, 256, 512)
+            if nxt:
+                hist_turn(nxt, 1)
+                self_term(nxt, 0)
+                self_term(nxt, 1)
+            if i >= 1:
+                y_copy(i - 1, 2, "dve" if i <= 10 else "act")
+                y_copy(i - 1, 3, "dve" if i in (5, 7, 9) else "act")
+            if 1 <= i <= 6:
+                store_y(i - 1, 0, 4)
+            if i >= 7:
+                store_y(i - 1, 0, 1)
+                store_y(i - 1, 1, 2)
+            if 2 <= i <= 10:
+                store_words(i - 2)
+            if i == 10:
+                store_words(9)
+            if i >= 7:
+                store_y(i - 1, 2, 3)
+                store_y(i - 1, 3, 4)
+            if i == 5:
+                store_scales(0, 0)
+            if i == 7:
+                store_scales(0, 1)
+            if i == 10:
+                store_scales(1, 0)
+        i = UNITS - 1
+        y_quant(10)
+        store_words(10)
+        y_round(i, 0, 512, "dve")
+        for j in range(4):
+            y_turn(i, j)
+            y_copy(i, j, "act")
+            if j == 2:
+                y_quant(i)
+                store_words(i)
+                store_scales(1, 1)
+            store_y(i, j, j + 1)

@@ -24,8 +24,9 @@ UNITS = 12
 N_AY = 3
 N_Y = 5
 N_WORDS = 4
-ROW_GAIN, ROW_SW, ROW_BIAS, ROW_CB, ROW_US = 0, 6, 12, 18, 24
-N_COLS = 19
+ROW_GAIN, ROW_SW, ROW_BIAS = 0, 6, 12
+ROW_CB, ROW_US = 0, 8
+N_COLS = 18
 
 
 def tile_lowrank_diagonal_item_scores_k5_kernel(
@@ -40,15 +41,16 @@ def tile_lowrank_diagonal_item_scores_k5_kernel(
         def sbuf(name, shape, dtype):
             return sb.tile(shape, dtype, name=name, align_bytes=64)
 
-        a_words = sbuf("a_words", [P, G, 2 * U], U8)
+        a_words = [sbuf("a_words%d" % h, [P, G, 2 * HALF], U8) for h in range(2)]
         e_words = sbuf("e_words", [P, G, 2 * R], U8)
-        a_scales = sbuf("a_scales", [P, G, U], U8)
+        a_scales = [sbuf("a_scales%d" % h, [P, G, HALF], U8) for h in range(2)]
         e_scales = sbuf("e_scales", [P, G, R], U8)
-        dec_raw = sbuf("dec_raw", [P, 4, I], BF16)
+        dec_raw = [sbuf("dec_raw%d" % n, [P, 4, 2 * HALF], BF16) for n in range(3)]
         dec_stage = [sbuf("dec_stage%d" % n, [P, 4 * HALF], BF16) for n in range(2)]
         dec_codes = sbuf("dec_codes", [P, G, HALF], U32)
         dec_scales = sbuf("dec_scales", [P, G, HALF], U8)
-        hist = sbuf("hist", [P, 8, I], BF16)
+        hist0 = [sbuf("hist0_%d" % n, [P, 4, 2 * HALF], BF16) for n in range(3)]
+        hist1 = sbuf("hist1", [P, 4, I], BF16)
         h_rows = [sbuf("h_rows%d" % n, [P, R], BF16) for n in range(4)]
         h_stage = sbuf("h_stage", [P, 4 * HALF], BF16)
         h_codes = sbuf("h_codes", [P, U], U32)
@@ -61,6 +63,9 @@ def tile_lowrank_diagonal_item_scores_k5_kernel(
         ident = sbuf("ident", [P, P], F32)
         vec = sbuf("vec", [P, HALF], BF16)
         vec32 = sbuf("vec32", [P, 5 * P], F32)
+        ivec = sbuf("ivec", [P, HALF], BF16)
+        ivec32 = sbuf("ivec32", [P, HALF], F32)
+        cb_col = sbuf("cb_col", [P, 4], F32)
         cols = sbuf("cols", [P, 4, N_COLS], F32)
         neg_c = sbuf("neg_c", [P, 4, G], F32)
         us_col = sbuf("us_col", [P, 8], F32)
@@ -77,59 +82,58 @@ def tile_lowrank_diagonal_item_scores_k5_kernel(
 
         ctx.enter_context(tc.manual_schedule())
 
-        def load_words(tile, src, gs, c0, c1):
-            nc.sync.dma_start(out=tile[:, gs, c0:c1].bitcast(I32),
-                              in_=src[gs, :, c0:c1].rearrange("g p n -> p g n").bitcast(I32))
+        def load_words(tile, src, gs, c0):
+            nc.sync.dma_start(out=tile[:, gs, :].bitcast(I32),
+                              in_=src[gs, :, c0:c0 + 2 * HALF].rearrange("g p n -> p g n").bitcast(I32))
 
-        def load_scales(eng, tile, src, r, c0, c1):
-            eng.dma_start(out=tile[r:P:32, :, c0:c1].bitcast(I32),
-                          in_=src.rearrange("g (q r) n -> r q g n", r=4)[r][:, :, c0:c1].bitcast(I32))
+        def load_scales(tile, src, c0):
+            for r in range(4):
+                nc.sync.dma_start(out=tile[r:P:32].bitcast(I32),
+                                  in_=src.rearrange("g (q r) n -> r q g n", r=4)[r][:, :, c0:c0 + HALF].bitcast(I32))
 
-        def load_dec(g0, g1):
-            c = slice(g0 * HALF, g1 * HALF)
-            nc.sync.dma_start(out=dec_raw[:, :, c], in_=dec[:, c].rearrange("(p j) c -> p j c", j=4))
+        def load_dec(n):
+            c = slice(2 * HALF * n, 2 * HALF * (n + 1))
+            nc.sync.dma_start(out=dec_raw[n][:], in_=dec[:, c].rearrange("(p j) c -> p j c", j=4))
 
-        def load_hist(j0, j1, c0, c1):
-            nc.sync.dma_start(out=hist[:, j0:j1, c0:c1],
-                              in_=history[j0 * P:j1 * P, c0:c1].rearrange("(j q) c -> q j c", q=P))
+        def load_hist0(n):
+            c = slice(2 * HALF * n, 2 * HALF * (n + 1))
+            nc.sync.dma_start(out=hist0[n][:], in_=history[0:HALF, c].rearrange("(j q) c -> q j c", q=P))
 
+        for plane in (e_scales, a_scales[0]):
+            nc.vector.memset(plane[:].rearrange("p g n -> p (g n)").bitcast(I32), 0)
         nc.vector.memset(vec[:].bitcast(I32), 0)
-        nc.vector.memset(e_scales[:].rearrange("p g n -> p (g n)").bitcast(I32), 0)
-        nc.vector.memset(a_scales[:, :, 0:HALF].bitcast(I32), 0)
-        nc.vector.memset(a_scales[:, :, HALF:U].bitcast(I32), 0)
-        load_words(e_words, enc_words, slice(0, 1), 0, 2 * R)
-        load_words(a_words, hist_words, slice(0, 1), 0, U)
-        nc.gpsimd.dma_start(out=vec[ROW_CB:ROW_CB + 1, :], in_=code_bias.rearrange("(o n) -> o n", o=1))
-        nc.gpsimd.dma_start(out=vec[ROW_US:ROW_US + 8, 0:P], in_=user_scale.rearrange("(j q) -> j q", q=P))
-        for row, src in ((ROW_GAIN, item_gain), (ROW_SW, self_weight), (ROW_BIAS, item_bias)):
-            nc.gpsimd.dma_start(out=vec[row:row + G, :], in_=src.rearrange("(g n) -> g n", n=HALF))
+        nc.vector.memset(ivec[:].bitcast(I32), 0)
+        nc.vector.memset(a_scales[1][:].rearrange("p g n -> p (g n)").bitcast(I32), 0)
         make_identity(nc, ident[:])
-        for r in range(4):
-            load_scales(nc.sync, e_scales, enc_scales, r, 0, R)
-        for r in range(4):
-            load_scales(nc.sync, a_scales, hist_scales, r, 0, HALF)
+        load_words(e_words, enc_words, slice(0, 1), 0)
+        load_words(a_words[0], hist_words, slice(0, 1), 0)
+        load_scales(e_scales, enc_scales, 0)
+        load_scales(a_scales[0], hist_scales, 0)
+        nc.sync.dma_start(out=vec[ROW_CB:ROW_CB + 1, :], in_=code_bias.rearrange("(o n) -> o n", o=1))
+        nc.sync.dma_start(out=vec[ROW_US:ROW_US + 8, 0:P], in_=user_scale.rearrange("(j q) -> j q", q=P))
         for gs in (slice(1, 3), slice(3, 6)):
-            load_words(e_words, enc_words, gs, 0, 2 * R)
-            load_words(a_words, hist_words, gs, 0, U)
-        for r in range(4):
-            load_scales(nc.gpsimd, a_scales, hist_scales, r, HALF, U)
-        load_dec(0, 2)
-        load_hist(0, 4, 0, 1024)
-        load_hist(0, 4, 1024, 2048)
-        load_words(a_words, hist_words, slice(0, 6), U, 2 * U)
-        load_dec(2, 4)
-        load_hist(0, 4, 2048, I)
-        load_dec(4, 6)
-        for j in range(4, 8):
-            load_hist(j, j + 1, 0, I)
+            load_words(e_words, enc_words, gs, 0)
+            load_words(a_words[0], hist_words, gs, 0)
+        load_dec(0)
+        for row, src in ((ROW_GAIN, item_gain), (ROW_SW, self_weight), (ROW_BIAS, item_bias)):
+            nc.sync.dma_start(out=ivec[row:row + G, :], in_=src.rearrange("(g n) -> g n", n=HALF))
+        load_hist0(0)
+        load_hist0(1)
+        load_scales(a_scales[1], hist_scales, HALF)
+        load_words(a_words[1], hist_words, slice(0, G), 2 * HALF)
+        load_dec(1)
+        load_hist0(2)
+        load_dec(2)
+        for j in range(4):
+            nc.sync.dma_start(out=hist1[:, j, :], in_=history[HALF + P * j:HALF + P * (j + 1), :])
 
         def encode(j, gs):
             if gs[0] == 0:
                 take(("enc", j))
             for g in gs:
                 nc.tensor.matmul_mx(
-                    out=bank_of["enc", j][:], lhsT=a_words[:, g, 2 * P * j:2 * P * (j + 1)].bitcast(FP4X4),
-                    lhsT_scale=a_scales[:, g, P * j:P * (j + 1)], rhs=e_words[:, g, :].bitcast(FP4X4),
+                    out=bank_of["enc", j][:], lhsT=a_words[j // 4][:, g, 2 * P * (j % 4):2 * P * (j % 4 + 1)].bitcast(FP4X4),
+                    lhsT_scale=a_scales[j // 4][:, g, P * (j % 4):P * (j % 4 + 1)], rhs=e_words[:, g, :].bitcast(FP4X4),
                     rhs_scale=e_scales[:, g, :], start=(g == 0), stop=(g == G - 1))
 
         def h_finish(j):
@@ -160,7 +164,7 @@ def tile_lowrank_diagonal_item_scores_k5_kernel(
 
         def dec_lay(g, eng, t0=0, t1=4):
             dst = dec_stage[g % 2][:].rearrange("p (t m j) -> p t m j", t=4, j=4)[:, t0:t1]
-            src = dec_raw[:, :, g * HALF:(g + 1) * HALF].rearrange("p j (m t) -> p t m j", t=4)[:, t0:t1]
+            src = dec_raw[g // 2][:, :, g % 2 * HALF:(g % 2 + 1) * HALF].rearrange("p j (m t) -> p t m j", t=4)[:, t0:t1]
             if eng == "pool":
                 nc.gpsimd.tensor_scalar(out=dst, in0=src, scalar1=1.0, scalar2=0.0, op0=MULT, op1=ADD)
             elif eng == "act":
@@ -174,9 +178,9 @@ def tile_lowrank_diagonal_item_scores_k5_kernel(
         def hist_turn(i, u):
             h, g = divmod(i, G)
             bank = take(("hist", i, u))
-            words = hist[:].bitcast(F32)
+            words, c = (hist1, g) if h else (hist0[g // 2], g % 2)
             for j in range(4):
-                nc.tensor.transpose(bank[:, P * j:P * (j + 1)], words[:, 4 * h + j, 256 * g + u:256 * (g + 1):2], ident[:])
+                nc.tensor.transpose(bank[:, P * j:P * (j + 1)], words[:].bitcast(F32)[:, j, 256 * c + u:256 * (c + 1):2], ident[:])
 
         def self_term(i, t, eng="act"):
             g = i % G
@@ -252,46 +256,53 @@ def tile_lowrank_diagonal_item_scores_k5_kernel(
                 nc.sync.dma_start(out=out_2[g0:g0 + n, 4 * q:4 * q + 4, HALF * h:HALF * (h + 1)].bitcast(I32),
                                   in_=y_scales[2 * h + part][32 * q:32 * q + 4 * n, :].bitcast(I32))
 
-        for g in (0, 1):
-            for j in range(4):
-                encode(j, [g])
+        for j in range(4):
+            encode(j, [0])
         nc.vector.tensor_copy(out=vec32[:, 0:HALF].rearrange("r (t m) -> r t m", t=4), in_=vec[:].rearrange("r (m t) -> r t m", t=4))
         nc.vector.tensor_copy(out=vec32[:, HALF:], in_=vec[:, 0:P])
         vb, ub = take("vec"), take("us")
         for t in range(4):
             nc.tensor.transpose(vb[:, P * t:P * (t + 1)], vec32[:, P * t:P * (t + 1)], ident[:])
         nc.tensor.transpose(ub[:, 0:P], vec32[:, HALF:], ident[:])
-        nc.vector.tensor_copy(out=cols[:], in_=vb[:].rearrange("p (t r) -> p t r", t=4)[:, :, 0:N_COLS])
+        nc.vector.tensor_copy(out=cb_col[:], in_=vb[:, ROW_CB:HALF:P])
         nc.vector.tensor_copy(out=us_col[:], in_=ub[:, ROW_US:ROW_US + 8])
         give("vec")
         give("us")
-        nc.vector.scalar_tensor_tensor(out=neg_c[:], in0=cols[:, :, ROW_SW:ROW_SW + G], scalar=-1.0,
-                                       in1=cols[:, :, ROW_GAIN:ROW_GAIN + G], op0=MULT, op1=MULT)
         for j in range(4):
-            encode(j, [2])
+            encode(j, [1])
         cbb = take("cb")
         for t in range(4):
-            nc.tensor.transpose(cbb[:, P * t:P * (t + 1)], cols[:, t, ROW_CB:ROW_CB + 1].to_broadcast([P, P]), ident[:])
+            nc.tensor.transpose(cbb[:, P * t:P * (t + 1)], cb_col[:, t:t + 1].to_broadcast([P, P]), ident[:])
         nc.scalar.activation(out=cb_rows[:].rearrange("q (u p e) -> q u p e", u=2, e=2),
                              in_=cbb[:].rearrange("q (u e p) -> q u p e", u=2, e=2), func=IDENT)
         give("cb")
+        for j in range(4):
+            encode(j, [2])
         encode(0, [3, 4, 5])
         encode(1, [3, 4, 5])
         h_finish(0)
         encode(2, [3, 4, 5])
         h_finish(1)
+        nc.scalar.copy(out=ivec32[:].rearrange("r (t m) -> r t m", t=4), in_=ivec[:].rearrange("r (m t) -> r t m", t=4))
         dec_lay(0, "dve")
         dec_lay(1, "act", 0, 2)
         h_turn(0)
         h_turn(1)
+        ib = take("ivec")
+        for t in range(4):
+            nc.tensor.transpose(ib[:, P * t:P * (t + 1)], ivec32[:, P * t:P * (t + 1)], ident[:])
         h_copy(0)
         h_copy(1)
+        nc.scalar.copy(out=cols[:], in_=ib[:].rearrange("p (t r) -> p t r", t=4)[:, :, 0:N_COLS])
+        give("ivec")
         dec_lay(1, "act", 2, 4)
         encode(3, [3, 4, 5])
         h_finish(2)
         h_quant(0)
         h_finish(3)
         h_quant(1)
+        nc.vector.scalar_tensor_tensor(out=neg_c[:], in0=cols[:, :, ROW_SW:ROW_SW + G], scalar=-1.0,
+                                       in1=cols[:, :, ROW_GAIN:ROW_GAIN + G], op0=MULT, op1=MULT)
         dec_quant(0)
         h_turn(2)
         h_copy(2)
@@ -340,9 +351,6 @@ def tile_lowrank_diagonal_item_scores_k5_kernel(
                 dec_lay(i + 1, "dve", 0, 2)
                 h_quant(3 + i)
                 dec_quant(i + 1)
-            if i == 10:
-                y_quant(8)
-                y_quant(9)
             if not mixed:
                 finish(i, 3)
             if i >= 1:
@@ -351,13 +359,10 @@ def tile_lowrank_diagonal_item_scores_k5_kernel(
                 y_turn(i - 1, 3)
             if mixed:
                 finish(i, 3)
-            if 2 <= i <= 9:
+            if i >= 2:
                 y_quant(i - 2)
-            if i < 10:
+            if i < UNITS - 1:
                 y_round(i)
-            if i == 10:
-                y_round(i, 0, 256)
-                y_round(i, 256, 512)
             if nxt:
                 hist_turn(nxt, 1)
                 self_term(nxt, 0)
@@ -372,16 +377,16 @@ def tile_lowrank_diagonal_item_scores_k5_kernel(
                 store_y(i - 1, 1, 2)
             if 2 <= i <= 10:
                 store_words(i - 2)
-            if i == 10:
-                store_words(9)
             if i >= 7:
                 store_y(i - 1, 2, 3)
                 store_y(i - 1, 3, 4)
+            if i == 11:
+                store_words(i - 2)
             if i == 5:
                 store_scales(0, 0)
             if i == 7:
                 store_scales(0, 1)
-            if i == 10:
+            if i == 11:
                 store_scales(1, 0)
         i = UNITS - 1
         y_quant(10)
@@ -390,8 +395,7 @@ def tile_lowrank_diagonal_item_scores_k5_kernel(
         for j in range(4):
             y_turn(i, j)
             y_copy(i, j, "act")
-            if j == 2:
-                y_quant(i)
-                store_words(i)
-                store_scales(1, 1)
             store_y(i, j, j + 1)
+        y_quant(i)
+        store_words(i)
+        store_scales(1, 1)

@@ -21,9 +21,10 @@ P = 128
 G = 6
 HALF = 512
 UNITS = 12
-N_AY = 3
-N_Y = 5
+N_AY = 4
+PAIRED = 8
 N_WORDS = 4
+LIGHT = (5, 6)
 ROW_GAIN, ROW_SW, ROW_BIAS = 0, 6, 12
 ROW_CB, ROW_US = 0, 8
 N_COLS = 18
@@ -59,7 +60,7 @@ def tile_lowrank_diagonal_item_scores_k5_kernel(
         y_stage = [sbuf("y_stage%d" % n, [P, 4 * HALF], BF16) for n in range(3)]
         y_words = [sbuf("y_words%d" % n, [P, HALF], U32) for n in range(N_WORDS)]
         y_scales = [sbuf("y_scales%d" % n, [P, HALF], U8) for n in range(4)]
-        y_rows = [sbuf("y_rows%d" % n, [P, 4, HALF], F32) for n in range(N_Y)]
+        y_rows = [sbuf("y_rows%d" % n, [P, 4, 2 * HALF], F32) for n in range(2)]
         ident = sbuf("ident", [P, P], F32)
         vec = sbuf("vec", [P, HALF], BF16)
         vec32 = sbuf("vec32", [P, 5 * P], F32)
@@ -215,7 +216,7 @@ def tile_lowrank_diagonal_item_scores_k5_kernel(
                 nc.tensor.transpose(bank[:, P * t:P * (t + 1)], yt[i % N_AY][:, t, P * j:P * (j + 1)], ident[:])
 
         def y_copy(i, j, eng):
-            dst = y_rows[i % N_Y][:, j, :].rearrange("q (p t) -> q p t", t=4)
+            dst = y_rows[i // 2 % 2][:, j, i % 2 * HALF:(i % 2 + 1) * HALF].rearrange("q (p t) -> q p t", t=4)
             src = bank_of["y", i, j][:].rearrange("q (t p) -> q p t", t=4)
             if eng == "act":
                 nc.scalar.copy(out=dst, in_=src)
@@ -238,11 +239,17 @@ def tile_lowrank_diagonal_item_scores_k5_kernel(
             nc.vector.quantize_mx(out=y_words[i % N_WORDS][:, m0:m1].bitcast(FP8X4),
                                   scales=y_scales[2 * h + g // 4][4 * (g % 4):P, m0:m1], in_=y_stage[i % 3][:, 4 * m0:4 * m1])
 
-        def store_y(i, j0, j1):
+        def store_y(i, n, j):
             h, g = divmod(i, G)
             nc.sync.dma_start(
-                out=out_0[HALF * h + P * j0:HALF * h + P * j1, HALF * g:HALF * (g + 1)].rearrange("(j q) c -> q j c", q=P),
-                in_=y_rows[i % N_Y][:, j0:j1, :])
+                out=out_0[HALF * h + P * j:HALF * h + P * (j + 1), HALF * g:HALF * (g + n)],
+                in_=y_rows[i // 2 % 2][:, j, i % 2 * HALF:(i % 2 + n) * HALF])
+
+        def store_done(i, j):
+            if i >= PAIRED:
+                store_y(i, 1, j)
+            elif i % 2 == 1:
+                store_y(i - 1, 2, j)
 
         def store_words(i, m0=0, m1=HALF):
             h, g = divmod(i, G)
@@ -295,7 +302,6 @@ def tile_lowrank_diagonal_item_scores_k5_kernel(
         h_copy(1)
         nc.scalar.copy(out=cols[:], in_=ib[:].rearrange("p (t r) -> p t r", t=4)[:, :, 0:N_COLS])
         give("ivec")
-        dec_lay(1, "act", 2, 4)
         encode(3, [3, 4, 5])
         h_finish(2)
         h_quant(0)
@@ -310,76 +316,91 @@ def tile_lowrank_diagonal_item_scores_k5_kernel(
         h_turn(3)
         h_copy(3)
         hist_turn(0, 1)
+        hist_turn(1, 0)
         h_quant(2)
         h_quant(3)
-        dec_quant(1)
+        dec_lay(1, "dve", 2, 4)
         for t in range(4):
             self_term(0, t)
 
+        halves = [(k, u) for k in range(2, UNITS) for u in range(2)]
+        late = None
         for i in range(UNITS):
-            nxt = 2 if i == 0 else (i + 1 if 2 <= i < UNITS - 1 else None)
             mixed = 1 <= i <= 4
-            if mixed:
-                encode(3 + i, list(range(G)))
-            if i == 1 or i >= 3:
-                self_term(2 if i == 1 else i, 2)
-                self_term(2 if i == 1 else i, 3)
+            light = i in LIGHT
+            if late:
+                self_term(late[0], 2 * late[1])
+                self_term(late[0], 2 * late[1] + 1)
+            early = halves.pop(0) if halves else None
+            late = halves.pop(0) if halves and not light else None
             if mixed:
                 dec_lay(i + 1, "act", 2, 4)
-                h_finish(3 + i)
-            for t in range(4):
-                decode(i, t)
+            decode(i, 0)
+            decode(i, 1)
+            if i <= 4:
+                decode(i, 2)
+                decode(i, 3)
             if i == 0:
-                for u in range(2):
-                    hist_turn(1, u)
-                for t in range(4):
-                    self_term(1, t)
+                hist_turn(1, 1)
             finish(i, 0)
             finish(i, 1)
-            if mixed:
-                h_turn(3 + i)
-                h_copy(3 + i)
+            if i == 0:
+                self_term(1, 0)
+                self_term(1, 1)
             if i >= 1:
                 y_turn(i - 1, 0)
                 y_turn(i - 1, 1)
-            finish(i, 2)
-            if i >= 1:
                 y_copy(i - 1, 0, "act")
-            if nxt:
-                hist_turn(nxt, 0)
+            if early:
+                hist_turn(*early)
+            if i >= 5:
+                decode(i, 2)
+                decode(i, 3)
+            if mixed:
+                encode(3 + i, list(range(G)))
+            finish(i, 2)
+            if i == 0:
+                self_term(1, 2)
+                self_term(1, 3)
+                dec_quant(1)
             if mixed:
                 dec_lay(i + 1, "dve", 0, 2)
-                h_quant(3 + i)
+            if 2 <= i <= 5:
+                h_quant(2 + i)
+            if mixed:
                 dec_quant(i + 1)
-            if not mixed:
-                finish(i, 3)
+            finish(i, 3)
             if i >= 1:
                 y_copy(i - 1, 1, "act")
                 y_turn(i - 1, 2)
                 y_turn(i - 1, 3)
-            if mixed:
-                finish(i, 3)
             if i >= 2:
                 y_quant(i - 2)
             if i < UNITS - 1:
                 y_round(i)
-            if nxt:
-                hist_turn(nxt, 1)
-                self_term(nxt, 0)
-                self_term(nxt, 1)
+            if mixed:
+                h_finish(3 + i)
+            if late:
+                hist_turn(*late)
+            if early:
+                self_term(early[0], 2 * early[1])
+                self_term(early[0], 2 * early[1] + 1)
             if i >= 1:
                 y_copy(i - 1, 2, "dve" if i <= 10 else "act")
-                y_copy(i - 1, 3, "dve" if i in (5, 7, 9) else "act")
-            if 1 <= i <= 6:
-                store_y(i - 1, 0, 4)
-            if i >= 7:
-                store_y(i - 1, 0, 1)
-                store_y(i - 1, 1, 2)
+            if mixed:
+                h_turn(3 + i)
+            if i >= 1:
+                y_copy(i - 1, 3, "dve" if i in (7, 9) else "act")
+            if mixed:
+                h_copy(3 + i)
+            if i >= 1:
+                store_done(i - 1, 0)
+                store_done(i - 1, 1)
             if 2 <= i <= 10:
                 store_words(i - 2)
-            if i >= 7:
-                store_y(i - 1, 2, 3)
-                store_y(i - 1, 3, 4)
+            if i >= 1:
+                store_done(i - 1, 2)
+                store_done(i - 1, 3)
             if i == 11:
                 store_words(i - 2)
             if i == 5:
@@ -395,7 +416,7 @@ def tile_lowrank_diagonal_item_scores_k5_kernel(
         for j in range(4):
             y_turn(i, j)
             y_copy(i, j, "act")
-            store_y(i, j, j + 1)
+            store_done(i, j)
         y_quant(i)
         store_words(i)
         store_scales(1, 1)

@@ -100,16 +100,16 @@ def tile_lowrank_diagonal_item_scores_k5_kernel(
             c = slice(2 * HALF * n, 2 * HALF * (n + 1))
             nc.sync.dma_start(out=hist0[n][:], in_=history[0:HALF, c].rearrange("(j q) c -> q j c", q=P))
 
-        for plane in (e_scales, a_scales[0]):
+        for plane in (e_scales, a_scales[0], a_scales[1]):
             nc.vector.memset(plane[:].rearrange("p g n -> p (g n)").bitcast(I32), 0)
         nc.vector.memset(vec[:].bitcast(I32), 0)
         nc.vector.memset(ivec[:].bitcast(I32), 0)
-        nc.vector.memset(a_scales[1][:].rearrange("p g n -> p (g n)").bitcast(I32), 0)
         make_identity(nc, ident[:])
         load_words(e_words, enc_words, slice(0, 1), 0)
         load_words(a_words[0], hist_words, slice(0, 1), 0)
         load_scales(e_scales, enc_scales, 0)
         load_scales(a_scales[0], hist_scales, 0)
+        load_scales(a_scales[1], hist_scales, HALF)
         nc.sync.dma_start(out=vec[ROW_CB:ROW_CB + 1, :], in_=code_bias.rearrange("(o n) -> o n", o=1))
         nc.sync.dma_start(out=vec[ROW_US:ROW_US + 8, 0:P], in_=user_scale.rearrange("(j q) -> j q", q=P))
         for gs in (slice(1, 3), slice(3, 6)):
@@ -120,7 +120,6 @@ def tile_lowrank_diagonal_item_scores_k5_kernel(
             nc.sync.dma_start(out=ivec[row:row + G, :], in_=src.rearrange("(g n) -> g n", n=HALF))
         load_hist0(0)
         load_hist0(1)
-        load_scales(a_scales[1], hist_scales, HALF)
         load_words(a_words[1], hist_words, slice(0, G), 2 * HALF)
         load_dec(1)
         load_hist0(2)
@@ -327,19 +326,18 @@ def tile_lowrank_diagonal_item_scores_k5_kernel(
         late = None
         for i in range(UNITS):
             mixed = 1 <= i <= 4
-            light = i in LIGHT
+            if mixed:
+                encode(3 + i, list(range(G)))
             if late:
                 self_term(late[0], 2 * late[1])
                 self_term(late[0], 2 * late[1] + 1)
             early = halves.pop(0) if halves else None
-            late = halves.pop(0) if halves and not light else None
+            late = halves.pop(0) if halves and i not in LIGHT else None
             if mixed:
                 dec_lay(i + 1, "act", 2, 4)
-            decode(i, 0)
-            decode(i, 1)
-            if i <= 4:
-                decode(i, 2)
-                decode(i, 3)
+                h_finish(3 + i)
+            for t in range(4):
+                decode(i, t)
             if i == 0:
                 hist_turn(1, 1)
             finish(i, 0)
@@ -347,39 +345,37 @@ def tile_lowrank_diagonal_item_scores_k5_kernel(
             if i == 0:
                 self_term(1, 0)
                 self_term(1, 1)
+            if mixed:
+                h_turn(3 + i)
+                h_copy(3 + i)
             if i >= 1:
                 y_turn(i - 1, 0)
                 y_turn(i - 1, 1)
+            finish(i, 2)
+            if i >= 1:
                 y_copy(i - 1, 0, "act")
             if early:
                 hist_turn(*early)
-            if i >= 5:
-                decode(i, 2)
-                decode(i, 3)
-            if mixed:
-                encode(3 + i, list(range(G)))
-            finish(i, 2)
             if i == 0:
                 self_term(1, 2)
                 self_term(1, 3)
                 dec_quant(1)
             if mixed:
                 dec_lay(i + 1, "dve", 0, 2)
-            if 2 <= i <= 5:
-                h_quant(2 + i)
-            if mixed:
+                h_quant(3 + i)
                 dec_quant(i + 1)
-            finish(i, 3)
+            if not mixed:
+                finish(i, 3)
             if i >= 1:
                 y_copy(i - 1, 1, "act")
                 y_turn(i - 1, 2)
                 y_turn(i - 1, 3)
+            if mixed:
+                finish(i, 3)
             if i >= 2:
                 y_quant(i - 2)
             if i < UNITS - 1:
                 y_round(i)
-            if mixed:
-                h_finish(3 + i)
             if late:
                 hist_turn(*late)
             if early:
@@ -387,12 +383,7 @@ def tile_lowrank_diagonal_item_scores_k5_kernel(
                 self_term(early[0], 2 * early[1] + 1)
             if i >= 1:
                 y_copy(i - 1, 2, "dve" if i <= 10 else "act")
-            if mixed:
-                h_turn(3 + i)
-            if i >= 1:
                 y_copy(i - 1, 3, "dve" if i in (7, 9) else "act")
-            if mixed:
-                h_copy(3 + i)
             if i >= 1:
                 store_done(i - 1, 0)
                 store_done(i - 1, 1)

from contextlib import ExitStack

import concourse.mybir as mybir
from concourse.masks import make_identity

U, I, R = 1024, 3072, 512
FLOPS = 2 * U * I * R * 2

F32 = mybir.dt.float32
BF16 = mybir.dt.bfloat16
I32 = mybir.dt.int32
U32 = mybir.dt.uint32
U8 = mybir.dt.uint8
FP8X4 = mybir.dt.float8_e4m3fn_x4
FP4X4 = mybir.dt.float4_e2m1fn_x4
MULT = mybir.AluOpType.mult
ADD = mybir.AluOpType.add
IDENT = mybir.ActivationFunctionType.Identity

P = 128
G = 6
HALF = 512
UNITS = 12
N_AY = 4
PAIRED = 8
N_WORDS = 4
LIGHT = (5, 6)
ROW_GAIN, ROW_SW, ROW_BIAS = 0, 6, 12
ROW_CB, ROW_US = 0, 8
N_COLS = 18


def tile_lowrank_diagonal_item_scores_k5_kernel(
    tc, hist_words, hist_scales, enc_words, enc_scales, dec, user_scale, code_bias, history,
    self_weight, item_gain, item_bias, out_0, out_1, out_2,
):
    nc = tc.nc
    with ExitStack() as ctx:
        sb = ctx.enter_context(tc.tile_pool(name="sb", bufs=1))
        ps = ctx.enter_context(tc.psum_pool(name="ps", bufs=1))

        def sbuf(name, shape, dtype):
            return sb.tile(shape, dtype, name=name, align_bytes=64)

        a_words = [sbuf("a_words%d" % h, [P, G, 2 * HALF], U8) for h in range(2)]
        e_words = sbuf("e_words", [P, G, 2 * R], U8)
        a_scales = [sbuf("a_scales%d" % h, [P, G, HALF], U8) for h in range(2)]
        e_scales = sbuf("e_scales", [P, G, R], U8)
        dec_raw = [sbuf("dec_raw%d" % n, [P, 4, 2 * HALF], BF16) for n in range(3)]
        dec_stage = [sbuf("dec_stage%d" % n, [P, 4 * HALF], BF16) for n in range(2)]
        dec_codes = sbuf("dec_codes", [P, G, HALF], U32)
        dec_scales = sbuf("dec_scales", [P, G, HALF], U8)
        hist0 = [sbuf("hist0_%d" % n, [P, 4, 2 * HALF], BF16) for n in range(3)]
        hist1 = sbuf("hist1", [P, 4, I], BF16)
        h_rows = [sbuf("h_rows%d" % n, [P, R], BF16) for n in range(4)]
        h_stage = sbuf("h_stage", [P, 4 * HALF], BF16)
        h_codes = sbuf("h_codes", [P, U], U32)
        h_scales = sbuf("h_scales", [P, U], U8)
        yt = [sbuf("yt%d" % n, [P, 4, HALF], F32) for n in range(N_AY)]
        y_stage = [sbuf("y_stage%d" % n, [P, 4 * HALF], BF16) for n in range(3)]
        y_words = [sbuf("y_words%d" % n, [P, HALF], U32) for n in range(N_WORDS)]
        y_scales = [sbuf("y_scales%d" % n, [P, HALF], U8) for n in range(4)]
        y_rows = [sbuf("y_rows%d" % n, [P, 4, 2 * HALF], F32) for n in range(2)]
        ident = sbuf("ident", [P, P], F32)
        vec = sbuf("vec", [P, HALF], BF16)
        vec32 = sbuf("vec32", [P, 5 * P], F32)
        ivec = sbuf("ivec", [P, HALF], BF16)
        ivec32 = sbuf("ivec32", [P, HALF], F32)
        cb_col = sbuf("cb_col", [P, 4], F32)
        cols = sbuf("cols", [P, 4, N_COLS], F32)
        neg_c = sbuf("neg_c", [P, 4, G], F32)
        us_col = sbuf("us_col", [P, 8], F32)
        cb_rows = sbuf("cb_rows", [P, R], F32)
        banks = [ps.tile([P, HALF], F32, name="bank%d" % n) for n in range(8)]
        bank_of = {}

        def take(key):
            bank_of[key] = banks.pop(0)
            return bank_of[key]

        def give(key):
            banks.append(bank_of[key])

        ctx.enter_context(tc.manual_schedule())

        def load_words(tile, src, gs, c0):
            nc.sync.dma_start(out=tile[:, gs, :].bitcast(I32),
                              in_=src[gs, :, c0:c0 + 2 * HALF].rearrange("g p n -> p g n").bitcast(I32))

        def load_scales(tile, src, c0):
            for r in range(4):
                nc.sync.dma_start(out=tile[r:P:32].bitcast(I32),
                                  in_=src.rearrange("g (q r) n -> r q g n", r=4)[r][:, :, c0:c0 + HALF].bitcast(I32))

        def load_dec(n):
            c = slice(2 * HALF * n, 2 * HALF * (n + 1))
            nc.sync.dma_start(out=dec_raw[n][:], in_=dec[:, c].rearrange("(p j) c -> p j c", j=4))

        def load_hist0(n):
            c = slice(2 * HALF * n, 2 * HALF * (n + 1))
            nc.sync.dma_start(out=hist0[n][:], in_=history[0:HALF, c].rearrange("(j q) c -> q j c", q=P))

        for plane in (e_scales, a_scales[0], a_scales[1]):
            nc.vector.memset(plane[:].rearrange("p g n -> p (g n)").bitcast(I32), 0)
        nc.vector.memset(vec[:].bitcast(I32), 0)
        nc.vector.memset(ivec[:].bitcast(I32), 0)
        make_identity(nc, ident[:])
        load_words(e_words, enc_words, slice(0, 1), 0)
        load_words(a_words[0], hist_words, slice(0, 1), 0)
        load_scales(e_scales, enc_scales, 0)
        load_scales(a_scales[0], hist_scales, 0)
        load_scales(a_scales[1], hist_scales, HALF)
        nc.sync.dma_start(out=vec[ROW_CB:ROW_CB + 1, :], in_=code_bias.rearrange("(o n) -> o n", o=1))
        nc.sync.dma_start(out=vec[ROW_US:ROW_US + 8, 0:P], in_=user_scale.rearrange("(j q) -> j q", q=P))
        for gs in (slice(1, 3), slice(3, 6)):
            load_words(e_words, enc_words, gs, 0)
            load_words(a_words[0], hist_words, gs, 0)
        load_dec(0)
        for row, src in ((ROW_GAIN, item_gain), (ROW_SW, self_weight), (ROW_BIAS, item_bias)):
            nc.sync.dma_start(out=ivec[row:row + G, :], in_=src.rearrange("(g n) -> g n", n=HALF))
        load_hist0(0)
        load_hist0(1)
        load_words(a_words[1], hist_words, slice(0, G), 2 * HALF)
        load_dec(1)
        load_hist0(2)
        load_dec(2)
        for j in range(4):
            nc.sync.dma_start(out=hist1[:, j, :], in_=history[HALF + P * j:HALF + P * (j + 1), :])

        def encode(j, gs):
            if gs[0] == 0:
                take(("enc", j))
            for g in gs:
                nc.tensor.matmul_mx(
                    out=bank_of["enc", j][:], lhsT=a_words[j // 4][:, g, 2 * P * (j % 4):2 * P * (j % 4 + 1)].bitcast(FP4X4),
                    lhsT_scale=a_scales[j // 4][:, g, P * (j % 4):P * (j % 4 + 1)], rhs=e_words[:, g, :].bitcast(FP4X4),
                    rhs_scale=e_scales[:, g, :], start=(g == 0), stop=(g == G - 1))

        def h_finish(j):
            src = bank_of["enc", j][:].rearrange("q (p u e) -> q u p e", u=2, e=2)
            for u in range(2):
                c = slice(256 * u, 256 * (u + 1))
                nc.vector.scalar_tensor_tensor(
                    out=h_rows[j % 4][:, c].rearrange("q (p e) -> q p e", e=2), in0=src[:, u],
                    scalar=us_col[:, j:j + 1], in1=cb_rows[:, c].rearrange("q (p e) -> q p e", e=2),
                    op0=MULT, op1=ADD)
            give(("enc", j))

        def h_turn(j):
            bank = take(("ht", j))
            for u in range(2):
                nc.tensor.transpose(bank[:, P * u:P * (u + 1)], h_rows[j % 4][:].bitcast(F32)[:, P * u:P * (u + 1)], ident[:])

        def h_copy(j, copy=nc.scalar.copy):
            c = slice(HALF * (j % 4), HALF * (j % 4 + 1))
            copy(out=h_stage[:, c].bitcast(F32).rearrange("p (r u) -> p r u", u=2),
                           in_=bank_of["ht", j][:, 0:2 * P].rearrange("p (u r) -> p r u", u=2))
            give(("ht", j))

        def h_quant(j):
            c = slice(HALF * (j % 4), HALF * (j % 4 + 1))
            nc.vector.quantize_mx(out=h_codes[:, P * j:P * (j + 1)].bitcast(FP8X4),
                                  scales=h_scales[:, P * j:P * (j + 1)], in_=h_stage[:, c])

        def dec_lay(g, eng, t0=0, t1=4):
            dst = dec_stage[g % 2][:].rearrange("p (t m j) -> p t m j", t=4, j=4)[:, t0:t1]
            src = dec_raw[g // 2][:, :, g % 2 * HALF:(g % 2 + 1) * HALF].rearrange("p j (m t) -> p t m j", t=4)[:, t0:t1]
            if eng == "pool":
                nc.gpsimd.tensor_scalar(out=dst, in0=src, scalar1=1.0, scalar2=0.0, op0=MULT, op1=ADD)
            elif eng == "act":
                nc.scalar.copy(out=dst, in_=src)
            else:
                nc.vector.tensor_copy(out=dst, in_=src)

        def dec_quant(g):
            nc.vector.quantize_mx(out=dec_codes[:, g, :].bitcast(FP8X4), scales=dec_scales[:, g, :], in_=dec_stage[g % 2][:])

        def hist_turn(i, u):
            h, g = divmod(i, G)
            bank = take(("hist", i, u))
            words, c = (hist1, g) if h else (hist0[g // 2], g % 2)
            for j in range(4):
                nc.tensor.transpose(bank[:, P * j:P * (j + 1)], words[:].bitcast(F32)[:, j, 256 * c + u:256 * (c + 1):2], ident[:])

        def self_term(i, t, eng="act"):
            g = i % G
            src = bank_of["hist", i, t // 2][:].bitcast(BF16)[:, t % 2:2 * HALF:2]
            dst = yt[i % N_AY][:, t, :]
            if eng == "act":
                nc.scalar.activation(out=dst, in_=src, func=IDENT, bias=cols[:, t, ROW_BIAS + g:ROW_BIAS + g + 1],
                                     scale=neg_c[:, t, g:g + 1])
            else:
                nc.vector.tensor_scalar(out=dst, in0=src, scalar1=neg_c[:, t, g:g + 1],
                                        scalar2=cols[:, t, ROW_BIAS + g:ROW_BIAS + g + 1], op0=MULT, op1=ADD)
            if t % 2 == 1:
                give(("hist", i, t // 2))

        def decode(i, t):
            h, g = divmod(i, G)
            nc.tensor.matmul_mx(
                out=take(("z", i, t))[:], lhsT=dec_codes[:, g, P * t:P * (t + 1)].bitcast(FP8X4),
                lhsT_scale=dec_scales[:, g, P * t:P * (t + 1)], rhs=h_codes[:, HALF * h:HALF * (h + 1)].bitcast(FP8X4),
                rhs_scale=h_scales[:, HALF * h:HALF * (h + 1)], start=True, stop=True)

        def finish(i, t):
            g = i % G
            dst = yt[i % N_AY][:, t, :]
            nc.vector.scalar_tensor_tensor(out=dst, in0=bank_of["z", i, t][:], scalar=cols[:, t, ROW_GAIN + g:ROW_GAIN + g + 1],
                                           in1=dst, op0=MULT, op1=ADD)
            give(("z", i, t))

        def y_turn(i, j):
            bank = take(("y", i, j))
            for t in range(4):
                nc.tensor.transpose(bank[:, P * t:P * (t + 1)], yt[i % N_AY][:, t, P * j:P * (j + 1)], ident[:])

        def y_copy(i, j, eng):
            dst = y_rows[i // 2 % 2][:, j, i % 2 * HALF:(i % 2 + 1) * HALF].rearrange("q (p t) -> q p t", t=4)
            src = bank_of["y", i, j][:].rearrange("q (t p) -> q p t", t=4)
            if eng == "act":
                nc.scalar.copy(out=dst, in_=src)
            else:
                nc.vector.tensor_copy(out=dst, in_=src)
            give(("y", i, j))

        def y_round(i, m0=0, m1=HALF, eng="pool"):
            dst = y_stage[i % 3][:, 4 * m0:4 * m1].rearrange("p (m t) -> p m t", t=4)
            src = yt[i % N_AY][:, :, m0:m1].rearrange("p t m -> p m t")
            if eng == "pool":
                nc.gpsimd.tensor_scalar(out=dst, in0=src, scalar1=1.0, scalar2=0.0, op0=MULT, op1=ADD)
            elif eng == "act":
                nc.scalar.copy(out=dst, in_=src)
            else:
                nc.vector.tensor_copy(out=dst, in_=src)

        def y_quant(i, m0=0, m1=HALF):
            h, g = divmod(i, G)
            nc.vector.quantize_mx(out=y_words[i % N_WORDS][:, m0:m1].bitcast(FP8X4),
                                  scales=y_scales[2 * h + g // 4][4 * (g % 4):P, m0:m1], in_=y_stage[i % 3][:, 4 * m0:4 * m1])

        def store_y(i, n, j):
            h, g = divmod(i, G)
            nc.sync.dma_start(
                out=out_0[HALF * h + P * j:HALF * h + P * (j + 1), HALF * g:HALF * (g + n)],
                in_=y_rows[i // 2 % 2][:, j, i % 2 * HALF:(i % 2 + n) * HALF])

        def store_done(i, j):
            if i >= PAIRED:
                store_y(i, 1, j)
            elif i % 2 == 1:
                store_y(i - 1, 2, j)

        def store_words(i, m0=0, m1=HALF):
            h, g = divmod(i, G)
            nc.sync.dma_start(
                out=out_1[g].rearrange("p m t -> p (m t)")[:, 4 * (HALF * h + m0):4 * (HALF * h + m1)].bitcast(I32),
                in_=y_words[i % N_WORDS][:, m0:m1].bitcast(I32))

        def store_scales(h, part):
            g0, n = (0, 4) if part == 0 else (4, 2)
            for q in range(4):
                nc.sync.dma_start(out=out_2[g0:g0 + n, 4 * q:4 * q + 4, HALF * h:HALF * (h + 1)].bitcast(I32),
                                  in_=y_scales[2 * h + part][32 * q:32 * q + 4 * n, :].bitcast(I32))

        for j in range(4):
            encode(j, [0])
        nc.vector.tensor_copy(out=vec32[:, 0:HALF].rearrange("r (t m) -> r t m", t=4), in_=vec[:].rearrange("r (m t) -> r t m", t=4))
        nc.vector.tensor_copy(out=vec32[:, HALF:], in_=vec[:, 0:P])
        vb, ub = take("vec"), take("us")
        for t in range(4):
            nc.tensor.transpose(vb[:, P * t:P * (t + 1)], vec32[:, P * t:P * (t + 1)], ident[:])
        nc.tensor.transpose(ub[:, 0:P], vec32[:, HALF:], ident[:])
        nc.vector.tensor_copy(out=cb_col[:], in_=vb[:, ROW_CB:HALF:P])
        nc.vector.tensor_copy(out=us_col[:], in_=ub[:, ROW_US:ROW_US + 8])
        give("vec")
        give("us")
        for j in range(4):
            encode(j, [1])
        cbb = take("cb")
        for t in range(4):
            nc.tensor.transpose(cbb[:, P * t:P * (t + 1)], cb_col[:, t:t + 1].to_broadcast([P, P]), ident[:])
        nc.scalar.activation(out=cb_rows[:].rearrange("q (u p e) -> q u p e", u=2, e=2),
                             in_=cbb[:].rearrange("q (u e p) -> q u p e", u=2, e=2), func=IDENT)
        give("cb")
        for j in range(4):
            encode(j, [2])
        encode(0, [3, 4, 5])
        encode(1, [3, 4, 5])
        h_finish(0)
        encode(2, [3, 4, 5])
        h_finish(1)
        nc.scalar.copy(out=ivec32[:].rearrange("r (t m) -> r t m", t=4), in_=ivec[:].rearrange("r (m t) -> r t m", t=4))
        dec_lay(0, "dve")
        dec_lay(1, "act", 0, 2)
        h_turn(0)
        h_turn(1)
        ib = take("ivec")
        for t in range(4):
            nc.tensor.transpose(ib[:, P * t:P * (t + 1)], ivec32[:, P * t:P * (t + 1)], ident[:])
        h_copy(0)
        h_copy(1)
        nc.scalar.copy(out=cols[:], in_=ib[:].rearrange("p (t r) -> p t r", t=4)[:, :, 0:N_COLS])
        give("ivec")
        encode(3, [3, 4, 5])
        h_finish(2)
        h_quant(0)
        h_finish(3)
        h_quant(1)
        nc.vector.scalar_tensor_tensor(out=neg_c[:], in0=cols[:, :, ROW_SW:ROW_SW + G], scalar=-1.0,
                                       in1=cols[:, :, ROW_GAIN:ROW_GAIN + G], op0=MULT, op1=MULT)
        dec_quant(0)
        h_turn(2)
        h_copy(2)
        hist_turn(0, 0)
        h_turn(3)
        h_copy(3)
        hist_turn(0, 1)
        hist_turn(1, 0)
        h_quant(2)
        h_quant(3)
        dec_lay(1, "dve", 2, 4)
        for t in range(4):
            self_term(0, t)

        halves = [(k, u) for k in range(2, UNITS) for u in range(2)]
        late = None
        for i in range(UNITS):
            mixed = 1 <= i <= 4
            if mixed:
                encode(3 + i, list(range(G)))
            if late:
                self_term(late[0], 2 * late[1])
                self_term(late[0], 2 * late[1] + 1)
            early = halves.pop(0) if halves else None
            late = halves.pop(0) if halves and i not in LIGHT else None
            if mixed:
                dec_lay(i + 1, "act", 2, 4)
                h_finish(3 + i)
            for t in range(4):
                decode(i, t)
            if i == 0:
                hist_turn(1, 1)
            finish(i, 0)
            finish(i, 1)
            if i == 0:
                self_term(1, 0)
                self_term(1, 1)
            if mixed:
                h_turn(3 + i)
                h_copy(3 + i)
            if i >= 1:
                y_turn(i - 1, 0)
                y_turn(i - 1, 1)
            finish(i, 2)
            if i >= 1:
                y_copy(i - 1, 0, "act")
            if early:
                hist_turn(*early)
            if i == 0:
                self_term(1, 2)
                self_term(1, 3)
                dec_quant(1)
            if mixed:
                dec_lay(i + 1, "dve", 0, 2)
                h_quant(3 + i)
                dec_quant(i + 1)
            if not mixed:
                finish(i, 3)
            if i >= 1:
                y_copy(i - 1, 1, "act")
                y_turn(i - 1, 2)
                y_turn(i - 1, 3)
            if mixed:
                finish(i, 3)
            if i >= 2:
                y_quant(i - 2)
            if i < UNITS - 1:
                y_round(i)
            if late:
                hist_turn(*late)
            if early:
                self_term(early[0], 2 * early[1])
                self_term(early[0], 2 * early[1] + 1)
            if i >= 1:
                y_copy(i - 1, 2, "dve" if i <= 10 else "act")
                y_copy(i - 1, 3, "dve" if i in (7, 9) else "act")
            if i >= 1:
                store_done(i - 1, 0)
                store_done(i - 1, 1)
            if 2 <= i <= 10:
                store_words(i - 2)
            if i >= 1:
                store_done(i - 1, 2)
                store_done(i - 1, 3)
            if i == 11:
                store_words(i - 2)
            if i == 5:
                store_scales(0, 0)
            if i == 7:
                store_scales(0, 1)
            if i == 11:
                store_scales(1, 0)
        i = UNITS - 1
        y_quant(10)
        store_words(10)
        y_round(i, 0, 512, "dve")
        for j in range(4):
            y_turn(i, j)
            y_copy(i, j, "act")
            store_done(i, j)
        y_quant(i)
        store_words(i)
        store_scales(1, 1)
